import numpy as np
import ml_dtypes


def mxq(x, axis, fmt="e4m3"):
    dtype, down = {"e4m3": (ml_dtypes.float8_e4m3fn, 7), "e5m2": (ml_dtypes.float8_e5m2, 14)}[fmt]
    v = np.moveaxis(np.asarray(x, np.float32).astype(ml_dtypes.bfloat16).astype(np.float64), axis, -1)
    blocks = v.reshape(v.shape[:-1] + (-1, 32))
    amax = np.abs(blocks).max(-1, keepdims=True)
    byte = np.maximum(np.where(amax > 0, np.frexp(amax)[1] - 1 + 127, 0) - down, 1)
    scale = np.exp2(byte - 127.0)
    codes = (blocks / scale).astype(np.float32).astype(dtype).astype(np.float64)
    return np.moveaxis((codes * scale).reshape(v.shape), -1, axis)


WIDE = False


def mx_kscale(k):
    if not WIDE:
        return np.ones(k)
    levels = np.array([10, -10, 5, -5, 0])
    if k % 512:
        return np.exp2(np.random.permutation(np.resize(levels, k // 32))).repeat(32)
    a = np.empty((k // 512, 16))
    for p in range(k // 512):
        a[p, :8] = np.random.permutation(np.resize(levels, 8))
        for g in range(8):
            far = levels[np.abs(levels - a[p, g]) >= 10]
            a[p, g + 8] = far[np.random.randint(len(far))]
    return np.exp2(a.ravel()).repeat(32)


def f64(x):
    return np.asarray(x).astype(np.float64)


def striped(idx):
    return np.tile(np.asarray(idx).reshape(-1, 16).T, (8, 1)).astype(np.uint16)


def unstriped(offs):
    return offs[:16].T.reshape(-1).astype(np.int64)


E2M1 = np.array([0.0, 0.5, 1.0, 1.5, 2.0, 3.0, 4.0, 6.0, -0.0, -0.5, -1.0, -1.5, -2.0, -3.0, -4.0, -6.0])


def pack_weight(w, fmt):
    k, n = w.shape
    w = f64(np.asarray(w, np.float32).astype(ml_dtypes.bfloat16)).reshape(k // 32, 32, n)
    amax = np.abs(w).max(1)
    if fmt == "e4m3":
        byte = np.frexp(amax)[1] - 1 + 127 - 7
    else:
        mant, ex = np.frexp(amax / 6.0)
        byte = np.where(mant > 0.5, ex, ex - 1) + 127
    byte = np.clip(np.where(amax > 0, byte, 1), 1, 254)
    scaled = (w * np.exp2(127.0 - byte)[:, None, :]).reshape(k, n).astype(np.float32)
    by_word = np.ascontiguousarray(scaled.reshape(k // 512, 128, 4, n).transpose(0, 1, 3, 2))
    if fmt == "e4m3":
        words = by_word.astype(ml_dtypes.float8_e4m3fn).view(np.uint8)
    else:
        c = by_word.astype(ml_dtypes.float4_e2m1fn).view(np.uint8) & 0xF
        words = (c[..., 0::2] | (c[..., 1::2] << 4)).reshape(k // 512, 128, 2 * n)
    return np.ascontiguousarray(words), np.ascontiguousarray(byte.astype(np.uint8).reshape(k // 512, 16, n))


def unpack_weight(words, scales, fmt):
    g, _, n = scales.shape
    words = np.ascontiguousarray(words).reshape(g, 128, n, -1)
    if fmt == "e4m3":
        vals = words.view(ml_dtypes.float8_e4m3fn).astype(np.float64)
    else:
        nib = np.empty((g, 128, n, 4), np.uint8)
        nib[..., 0::2] = words & 0xF
        nib[..., 1::2] = words >> 4
        vals = E2M1[nib]
    vals = vals * np.repeat(np.exp2(scales.astype(np.float64) - 127.0), 8, axis=1)[..., None]
    return vals.transpose(0, 1, 3, 2).reshape(g * 512, n)


K, B, T, I, Q = 512, 512, 2048, 512, 128


def setup_inputs():
    n = np.random.standard_normal
    idx = np.random.permutation(T)[:I]
    fk = mx_kscale(K)
    fi = mx_kscale(I)
    embp = pack_weight(n((K, T)) / fk[:, None], "e4m3")
    return {
        "qemb": (n((K, Q)) * fk[:, None]).astype(np.float32),
        "wq": (n((K, B)) * 1 / np.sqrt(K) / fk[:, None]).astype(np.float32),
        "emb_words": embp[0],
        "emb_scales": embp[1],
        "wi": (n((K, B)) * 1 / np.sqrt(K) * fk[:, None]).astype(np.float32),
        "isc": (np.random.uniform(0.5, 2.0, (I, 1)) * fi[:, None]).astype(np.float32),
        "dsc": (n((I, Q)) * 0.06 / fi[:, None]).astype(np.float32),
        "gain": (np.random.uniform(0.5, 2.0, (B, 1))).astype(np.float32),
        "old": (n((B, Q)) * 0.5).astype(np.float32),
        "offs": striped(idx),
    }


def reference(qemb, wq, emb_words, emb_scales, wi, isc, dsc, gain, old, offs):
    idx = unstriped(offs)
    embu = unpack_weight(emb_words, emb_scales, "e4m3")
    wqq = mxq(f64(wq), 0, "e4m3")
    qembq = mxq(f64(qemb), 0, "e4m3")
    z = wqq.T @ qembq
    wiq = mxq(f64(wi), 0, "e4m3")
    embidxg = embu[:, idx]
    g1 = wiq.T @ embidxg
    h1 = np.tanh(g1)
    ht = h1.T
    hs = ht * f64(isc)
    hsq = mxq(hs, 0, "e4m3")
    dscq = mxq(f64(dsc), 0, "e4m3")
    gh = hsq.T @ dscq
    y = gh * (1.0 - np.square(np.tanh(z))) * f64(gain) + f64(old)
    return y

@@ -1,0 +1,180 @@
+from contextlib import ExitStack
+
+import concourse.mybir as mybir
+from concourse.masks import make_identity
+
+K, B, T, I, Q = 512, 512, 2048, 512, 128
+FLOPS = 2 * (K * B * Q + K * B * I + I * B * Q)
+
+F32 = mybir.dt.float32
+BF16 = mybir.dt.bfloat16
+I32 = mybir.dt.int32
+U32 = mybir.dt.uint32
+U16 = mybir.dt.uint16
+U8 = mybir.dt.uint8
+FP8X4 = mybir.dt.float8_e4m3fn_x4
+ACT = mybir.ActivationFunctionType
+ALU = mybir.AluOpType
+
+P = 128
+PACK = 4
+CHUNKS = B // P
+HALF = B // 2
+
+
+def tile_attend_bsoftcodes_kernel(tc, qemb, wq, emb_words, emb_scales, wi, isc, dsc, gain, old, offs, out):
+    nc = tc.nc
+    with ExitStack() as ctx:
+        sb = ctx.enter_context(tc.tile_pool(name="sb", bufs=1))
+        ps = ctx.enter_context(tc.psum_pool(name="ps", bufs=1))
+
+        def load_rows(name, rows):
+            width = rows.shape[1]
+            raw = sb.tile([P, PACK, width], F32, name=name)
+            nc.sync.dma_start(raw[:], rows.rearrange("(p j) w -> p j w", j=PACK))
+            return raw
+
+        def interleave(name, raw, on_scalar):
+            width = raw.shape[2]
+            grouped = sb.tile([P, width * PACK], BF16, name=name, align_bytes=64)
+            dst = grouped[:].rearrange("p (c i j) -> p c j i", i=4, j=PACK)
+            src = raw.rearrange("p j (c i) -> p c j i", i=4)
+            if on_scalar:
+                nc.scalar.copy(dst, src)
+            else:
+                nc.vector.tensor_copy(dst, src)
+            return grouped
+
+        def quantize(name, grouped):
+            width = grouped.shape[1] // PACK
+            codes = sb.tile([P, width], U32, name=name + "_codes", align_bytes=64)
+            scales = sb.tile([P, width], U8, name=name + "_scales", align_bytes=64)
+            nc.vector.quantize_mx(out=codes[:].bitcast(FP8X4), scales=scales[:], in_=grouped[:])
+            return codes, scales
+
+        def product(acc, left, left_cols, right, right_cols):
+            nc.tensor.matmul_mx(
+                out=acc,
+                lhsT=left[0][:, left_cols].bitcast(FP8X4),
+                lhsT_scale=left[1][:, left_cols],
+                rhs=right[0][:, right_cols].bitcast(FP8X4),
+                rhs_scale=right[1][:, right_cols],
+                start=True,
+                stop=True,
+            )
+
+        whole = slice(0, P)
+
+        offsets = sb.tile([P, I // 16], U16, name="offsets")
+        nc.sync.dma_start(offsets[:], offs)
+        store_scales = sb.tile([P, T], U8, name="store_scales")
+        nc.vector.memset(store_scales[:].bitcast(I32), 0)
+        for quad in range(4):
+            nc.scalar.dma_start(
+                store_scales[32 * quad : 32 * quad + 4, :].bitcast(I32),
+                emb_scales[0, 4 * quad : 4 * quad + 4, :].bitcast(I32),
+            )
+        store_words = sb.tile([P, T], U32, name="store_words")
+        nc.sync.dma_start(store_words[:].bitcast(I32), emb_words[0].rearrange("p n t -> p (n t)").bitcast(I32))
+        wi_raw = [load_rows("wi_raw%d" % h, wi[:, h * HALF : (h + 1) * HALF]) for h in range(2)]
+        dsc_raw = load_rows("dsc_raw", dsc)
+        qemb_raw = load_rows("qemb_raw", qemb)
+        wq_raw = [load_rows("wq_raw%d" % h, wq[:, h * HALF : (h + 1) * HALF]) for h in range(2)]
+        old_sb = sb.tile([P, CHUNKS, Q], F32, name="old_sb")
+        nc.sync.dma_start(old_sb[:], old.rearrange("(c p) q -> p c q", p=P))
+
+        slot_scale = sb.tile([P, PACK], F32, name="slot_scale")
+        nc.gpsimd.dma_start(slot_scale[:], isc.rearrange("(p r) o -> p (r o)", r=PACK))
+        gain_rows = sb.tile([P, P], F32, name="gain_rows")
+        nc.gpsimd.memset(gain_rows[:], 0.0)
+        nc.gpsimd.dma_start(gain_rows[0:CHUNKS, :], gain.rearrange("(c p) o -> c (p o)", p=P))
+        identity = sb.tile([P, P], F32, name="identity")
+        make_identity(nc, identity[:])
+
+        warm_in = sb.tile([P, 1], F32, name="warm_in")
+        nc.vector.memset(warm_in[:], 0.0)
+        warm_out = sb.tile([P, 1], F32, name="warm_out")
+        nc.scalar.activation(warm_out[:], warm_in[:], ACT.Tanh)
+
+        listed_scales = sb.tile([P, I], U8, name="listed_scales")
+        nc.vector.tensor_copy(listed_scales[:], store_scales[:].indirect(offsets[:]))
+        dealt_scales = sb.tile([P, I], U8, name="dealt_scales", align_bytes=64)
+        nc.vector.tensor_copy(
+            dealt_scales[:].rearrange("p (r s) -> p s r", r=PACK),
+            listed_scales[:].rearrange("p (s r) -> p s r", r=PACK),
+        )
+        dealt_words = sb.tile([P, I], U32, name="dealt_words", align_bytes=64)
+        nc.vector.tensor_copy(
+            dealt_words[:].rearrange("p (r s) -> p s r", r=PACK),
+            store_words[:].indirect(offsets[:]),
+        )
+        items = (dealt_words, dealt_scales)
+
+        wi_grouped = [interleave("wi_g%d" % c, wi_raw[0][:, :, c * P : (c + 1) * P], True) for c in range(2)]
+        wi_q = [quantize("wi%d" % c, wi_grouped[c]) for c in range(2)]
+        wi_grouped_b = interleave("wi_gb", wi_raw[1][:], False)
+        wi_q_b = quantize("wib", wi_grouped_b)
+        wi_ops = [(wi_q[0], whole), (wi_q[1], whole), (wi_q_b, slice(0, P)), (wi_q_b, slice(P, 2 * P))]
+
+        codes_f32 = []
+        for c in range(CHUNKS):
+            bank = ps.tile([P, PACK, P], F32, name="g1_%d" % c, tag="bank%d" % c)
+            for r in range(PACK):
+                product(bank[:, r, :], items, slice(r * P, (r + 1) * P), wi_ops[c][0], wi_ops[c][1])
+            h = sb.tile([P, P, PACK], F32, name="h%d" % c)
+            nc.scalar.activation(h[:], bank[:].rearrange("p r n -> p n r"), ACT.Tanh)
+            codes_f32.append(h)
+            if c == 1:
+                dsc_grouped = interleave("dsc_g", dsc_raw[:], True)
+        gain_ps = ps.tile([P, P], F32, name="gain_ps", tag="bank0")
+        nc.tensor.transpose(gain_ps[:], gain_rows[:], identity[:])
+        neg_gain = sb.tile([P, CHUNKS], F32, name="neg_gain")
+        nc.scalar.mul(neg_gain[:], gain_ps[:, 0:CHUNKS], -1.0)
+        qemb_grouped = interleave("qemb_g", qemb_raw[:], True)
+        wq_grouped = [interleave("wq_g0", wq_raw[0][:], True)]
+
+        scale_spread = slot_scale[:].unsqueeze(1).to_broadcast([P, P, PACK])
+        hs, hs_q = [], []
+        for c in range(CHUNKS):
+            scaled = sb.tile([P, P * PACK], BF16, name="hs%d" % c, align_bytes=64)
+            nc.vector.tensor_tensor(
+                scaled[:].rearrange("p (n r) -> p n r", r=PACK), codes_f32[c][:], scale_spread, ALU.mult
+            )
+            hs.append(scaled)
+            if c == 0:
+                dsc_q = quantize("dsc", dsc_grouped)
+            else:
+                hs_q.append(quantize("hs%d" % (c - 1), hs[c - 1]))
+        qemb_q = quantize("qemb", qemb_grouped)
+        hs_q.append(quantize("hs%d" % (CHUNKS - 1), hs[CHUNKS - 1]))
+
+        gh = []
+        for c in range(CHUNKS):
+            acc = ps.tile([P, Q], F32, name="gh_%d" % c, tag="bank%d" % c)
+            product(acc[:], hs_q[c], whole, dsc_q, whole)
+            gh.append(acc)
+
+        wq_q = [quantize("wq0", wq_grouped[0])]
+        wq_grouped.append(interleave("wq_g1", wq_raw[1][:], False))
+        for half in range(2):
+            if half == 1:
+                wq_q.append(quantize("wq1", wq_grouped[1]))
+            z = ps.tile([P, 2, Q], F32, name="z%d" % half)
+            for e in range(2):
+                product(z[:, e, :], wq_q[half], slice(e * P, (e + 1) * P), qemb_q, whole)
+            code = sb.tile([P, 2, Q], F32, name="code%d" % half)
+            nc.scalar.activation(code[:], z[:], ACT.Tanh)
+            square = sb.tile([P, 2, Q], F32, name="square%d" % half)
+            nc.scalar.activation(square[:], code[:], ACT.Square)
+            bent = [sb.tile([P, Q], F32, name="bent%d_%d" % (half, e)) for e in range(2)]
+            for e in range(2):
+                nc.vector.scalar_tensor_tensor(
+                    bent[e][:], square[:, e, :], 1.0, gh[2 * half + e][:], ALU.subtract, ALU.mult
+                )
+            for e in range(2):
+                c = 2 * half + e
+                result = sb.tile([P, Q], F32, name="result%d" % c)
+                nc.vector.scalar_tensor_tensor(
+                    result[:], bent[e][:], neg_gain[:, c : c + 1], old_sb[:, c, :], ALU.mult, ALU.add
+                )
+                nc.sync.dma_start(out[c * P : (c + 1) * P, :], result[:])

@@ -1,7 +1,6 @@
 from contextlib import ExitStack
 
 import concourse.mybir as mybir
-from concourse.masks import make_identity
 
 K, B, T, I, Q = 512, 512, 2048, 512, 128
 FLOPS = 2 * (K * B * Q + K * B * I + I * B * Q)
@@ -28,22 +27,22 @@ def tile_attend_bsoftcodes_kernel(tc, qemb, wq, emb_words, emb_scales, wi, isc, 
         sb = ctx.enter_context(tc.tile_pool(name="sb", bufs=1))
         ps = ctx.enter_context(tc.psum_pool(name="ps", bufs=1))
 
-        def load_rows(name, rows):
+        def load_rows(pool, name, rows, offset=None):
             width = rows.shape[1]
-            raw = sb.tile([P, PACK, width], F32, name=name)
+            raw = pool.tile([P, PACK, width], F32, name=name, offset=offset)
             nc.sync.dma_start(raw[:], rows.rearrange("(p j) w -> p j w", j=PACK))
             return raw
 
-        def interleave(name, raw, on_scalar):
-            width = raw.shape[2]
-            grouped = sb.tile([P, width * PACK], BF16, name=name, align_bytes=64)
-            dst = grouped[:].rearrange("p (c i j) -> p c j i", i=4, j=PACK)
-            src = raw.rearrange("p j (c i) -> p c j i", i=4)
-            if on_scalar:
-                nc.scalar.copy(dst, src)
-            else:
-                nc.vector.tensor_copy(dst, src)
-            return grouped
+        def grouped_tile(name, width):
+            return sb.tile([P, width * PACK], BF16, name=name, align_bytes=64)
+
+        def interleave(copy, grouped, raw):
+            copy(
+                grouped.rearrange("p (c i j) -> p c j i", i=2, j=PACK),
+                raw.rearrange("p j (c i) -> p c j i", i=2),
+            )
+
+        on_scalar, on_vector = nc.scalar.copy, nc.vector.tensor_copy
 
         def quantize(name, grouped):
             width = grouped.shape[1] // PACK
@@ -67,41 +66,48 @@ def tile_attend_bsoftcodes_kernel(tc, qemb, wq, emb_words, emb_scales, wi, isc, 
 
         offsets = sb.tile([P, I // 16], U16, name="offsets")
         nc.sync.dma_start(offsets[:], offs)
+        wi_raw = [load_rows(sb, "wi_raw0", wi[:, 0:HALF])]
         store_scales = sb.tile([P, T], U8, name="store_scales")
-        nc.vector.memset(store_scales[:].bitcast(I32), 0)
+        nc.gpsimd.memset(store_scales[:].bitcast(I32), 0)
         for quad in range(4):
-            nc.scalar.dma_start(
+            nc.sync.dma_start(
                 store_scales[32 * quad : 32 * quad + 4, :].bitcast(I32),
                 emb_scales[0, 4 * quad : 4 * quad + 4, :].bitcast(I32),
             )
-        store_words = sb.tile([P, T], U32, name="store_words")
-        nc.sync.dma_start(store_words[:].bitcast(I32), emb_words[0].rearrange("p n t -> p (n t)").bitcast(I32))
-        wi_raw = [load_rows("wi_raw%d" % h, wi[:, h * HALF : (h + 1) * HALF]) for h in range(2)]
-        dsc_raw = load_rows("dsc_raw", dsc)
-        qemb_raw = load_rows("qemb_raw", qemb)
-        wq_raw = [load_rows("wq_raw%d" % h, wq[:, h * HALF : (h + 1) * HALF]) for h in range(2)]
-        old_sb = sb.tile([P, CHUNKS, Q], F32, name="old_sb")
-        nc.sync.dma_start(old_sb[:], old.rearrange("(c p) q -> p c q", p=P))
-
-        slot_scale = sb.tile([P, PACK], F32, name="slot_scale")
-        nc.gpsimd.dma_start(slot_scale[:], isc.rearrange("(p r) o -> p (r o)", r=PACK))
-        gain_rows = sb.tile([P, P], F32, name="gain_rows")
-        nc.gpsimd.memset(gain_rows[:], 0.0)
-        nc.gpsimd.dma_start(gain_rows[0:CHUNKS, :], gain.rearrange("(c p) o -> c (p o)", p=P))
-        identity = sb.tile([P, P], F32, name="identity")
-        make_identity(nc, identity[:])
-
         warm_in = sb.tile([P, 1], F32, name="warm_in")
         nc.vector.memset(warm_in[:], 0.0)
         warm_out = sb.tile([P, 1], F32, name="warm_out")
         nc.scalar.activation(warm_out[:], warm_in[:], ACT.Tanh)
+        gain_rows = sb.tile([P, P], F32, name="gain_rows")
+        nc.vector.memset(gain_rows[:], 0.0)
+        nc.scalar.dma_start(gain_rows[0:CHUNKS, :], gain.rearrange("(c p) o -> c (p o)", p=P))
 
-        listed_scales = sb.tile([P, I], U8, name="listed_scales")
+        identity = sb.tile([P, P], F32, name="identity")
+        late = ctx.enter_context(tc.tile_pool(name="late", bufs=1))
+        zeros = late.tile([P, 6688], F32, name="zeros", offset=0)
+        nc.gpsimd.memset(zeros[:, 0:P], 0.0)
+        nc.gpsimd.affine_select(
+            out=identity[:], in_=zeros[:, 0:P], compare_op=ALU.not_equal, fill=1.0,
+            base=0, pattern=[[-1, P]], channel_multiplier=1,
+        )
+
+        store_words = late.tile([P, T], U32, name="store_words", offset=0)
+        nc.sync.dma_start(store_words[:].bitcast(I32), emb_words[0].rearrange("p n t -> p (n t)").bitcast(I32))
+        slot_scale = late.tile([P, PACK], F32, name="slot_scale", offset=26624)
+        nc.sync.dma_start(slot_scale[:], isc.rearrange("(p r) o -> p (r o)", r=PACK))
+        wi_raw.append(load_rows(late, "wi_raw1", wi[:, HALF:B], 8192))
+        qemb_raw = load_rows(late, "qemb_raw", qemb, 12288)
+        dsc_raw = load_rows(late, "dsc_raw", dsc, 14336)
+        wq_raw = [load_rows(late, "wq_raw%d" % h, wq[:, h * HALF : (h + 1) * HALF], 16384 + 4096 * h) for h in range(2)]
+        old_sb = late.tile([P, CHUNKS, Q], F32, name="old_sb", offset=24576)
+        nc.sync.dma_start(old_sb[:], old.rearrange("(c p) q -> p c q", p=P))
+
+        listed_scales = sb.tile([P, I], U8, name="listed_scales", align_bytes=64, tag="wi0_codes")
         nc.vector.tensor_copy(listed_scales[:], store_scales[:].indirect(offsets[:]))
         dealt_scales = sb.tile([P, I], U8, name="dealt_scales", align_bytes=64)
         nc.vector.tensor_copy(
-            dealt_scales[:].rearrange("p (r s) -> p s r", r=PACK),
-            listed_scales[:].rearrange("p (s r) -> p s r", r=PACK),
+            dealt_scales[:].rearrange("p (r s) -> p r s", r=PACK),
+            listed_scales[:].rearrange("p (s r) -> p r s", r=PACK),
         )
         dealt_words = sb.tile([P, I], U32, name="dealt_words", align_bytes=64)
         nc.vector.tensor_copy(
@@ -110,71 +116,86 @@ def tile_attend_bsoftcodes_kernel(tc, qemb, wq, emb_words, emb_scales, wi, isc, 
         )
         items = (dealt_words, dealt_scales)
 
-        wi_grouped = [interleave("wi_g%d" % c, wi_raw[0][:, :, c * P : (c + 1) * P], True) for c in range(2)]
-        wi_q = [quantize("wi%d" % c, wi_grouped[c]) for c in range(2)]
-        wi_grouped_b = interleave("wi_gb", wi_raw[1][:], False)
-        wi_q_b = quantize("wib", wi_grouped_b)
-        wi_ops = [(wi_q[0], whole), (wi_q[1], whole), (wi_q_b, slice(0, P)), (wi_q_b, slice(P, 2 * P))]
+        halves = [slice(0, P), slice(P, HALF)]
+        wi_grouped = [grouped_tile("wi_g0", HALF), grouped_tile("wi_g2", P), grouped_tile("wi_g3", P)]
+        interleave(on_scalar, wi_grouped[0][:], wi_raw[0][:])
+        for e in range(2):
+            interleave(on_scalar, wi_grouped[1 + e][:], wi_raw[1][:, :, halves[e]])
+        wi_first = quantize("wi0", wi_grouped[0])
+        wi_q = [(wi_first, cols) for cols in halves]
+        wi_q.extend((quantize("wi%d" % (2 + e), wi_grouped[1 + e]), whole) for e in range(2))
+        qemb_grouped = grouped_tile("qemb_g", Q)
+        interleave(on_scalar, qemb_grouped[:], qemb_raw[:])
+        qemb_q = quantize("qemb", qemb_grouped)
 
-        codes_f32 = []
-        for c in range(CHUNKS):
-            bank = ps.tile([P, PACK, P], F32, name="g1_%d" % c, tag="bank%d" % c)
-            for r in range(PACK):
-                product(bank[:, r, :], items, slice(r * P, (r + 1) * P), wi_ops[c][0], wi_ops[c][1])
-            h = sb.tile([P, P, PACK], F32, name="h%d" % c)
-            nc.scalar.activation(h[:], bank[:].rearrange("p r n -> p n r"), ACT.Tanh)
-            codes_f32.append(h)
-            if c == 1:
-                dsc_grouped = interleave("dsc_g", dsc_raw[:], True)
-        gain_ps = ps.tile([P, P], F32, name="gain_ps", tag="bank0")
+        gain_ps = ps.tile([P, P], F32, name="gain_ps")
         nc.tensor.transpose(gain_ps[:], gain_rows[:], identity[:])
         neg_gain = sb.tile([P, CHUNKS], F32, name="neg_gain")
         nc.scalar.mul(neg_gain[:], gain_ps[:, 0:CHUNKS], -1.0)
-        qemb_grouped = interleave("qemb_g", qemb_raw[:], True)
-        wq_grouped = [interleave("wq_g0", wq_raw[0][:], True)]
+
+        wq_grouped = [grouped_tile("wq_g%d" % h, HALF) for h in range(2)]
+        codes_f32 = []
+        for c in range(CHUNKS):
+            if c % 2 == 0:
+                interleave(on_scalar, wq_grouped[c // 2][:, 0 : P * PACK], wq_raw[c // 2][:, :, 0:P])
+            bank = ps.tile([P, PACK, P], F32, name="g1_%d" % c, tag="bank%d" % c)
+            for r in range(PACK):
+                product(bank[:, r, :], items, slice(r * P, (r + 1) * P), *wi_q[c])
+            if c < 2:
+                h = late.tile([P, P, PACK], F32, name="h%d" % c, offset=8192 + 2048 * c)
+            else:
+                h = sb.tile([P, P, PACK], F32, name="h%d" % c)
+            nc.scalar.activation(h[:], bank[:].rearrange("p r n -> p n r"), ACT.Tanh)
+            codes_f32.append(h)
 
         scale_spread = slot_scale[:].unsqueeze(1).to_broadcast([P, P, PACK])
-        hs, hs_q = [], []
-        for c in range(CHUNKS):
+        gh = [ps.tile([P, 2, Q], F32, name="gh_%d" % half, tag="bank%d" % half) for half in range(2)]
+
+        def scaled_codes(c):
             scaled = sb.tile([P, P * PACK], BF16, name="hs%d" % c, align_bytes=64)
             nc.vector.tensor_tensor(
                 scaled[:].rearrange("p (n r) -> p n r", r=PACK), codes_f32[c][:], scale_spread, ALU.mult
             )
-            hs.append(scaled)
-            if c == 0:
-                dsc_q = quantize("dsc", dsc_grouped)
-            else:
-                hs_q.append(quantize("hs%d" % (c - 1), hs[c - 1]))
-        qemb_q = quantize("qemb", qemb_grouped)
-        hs_q.append(quantize("hs%d" % (CHUNKS - 1), hs[CHUNKS - 1]))
+            return scaled
 
-        gh = []
-        for c in range(CHUNKS):
-            acc = ps.tile([P, Q], F32, name="gh_%d" % c, tag="bank%d" % c)
-            product(acc[:], hs_q[c], whole, dsc_q, whole)
-            gh.append(acc)
+        def slot_sum(c, scaled):
+            product(gh[c // 2][:, c % 2, :], quantize("hs%d" % c, scaled), whole, dsc_q, whole)
 
-        wq_q = [quantize("wq0", wq_grouped[0])]
-        wq_grouped.append(interleave("wq_g1", wq_raw[1][:], False))
-        for half in range(2):
-            if half == 1:
-                wq_q.append(quantize("wq1", wq_grouped[1]))
+        def query_squares(half, operands):
             z = ps.tile([P, 2, Q], F32, name="z%d" % half)
             for e in range(2):
-                product(z[:, e, :], wq_q[half], slice(e * P, (e + 1) * P), qemb_q, whole)
+                product(z[:, e, :], operands[e][0], operands[e][1], qemb_q, whole)
             code = sb.tile([P, 2, Q], F32, name="code%d" % half)
             nc.scalar.activation(code[:], z[:], ACT.Tanh)
             square = sb.tile([P, 2, Q], F32, name="square%d" % half)
             nc.scalar.activation(square[:], code[:], ACT.Square)
-            bent = [sb.tile([P, Q], F32, name="bent%d_%d" % (half, e)) for e in range(2)]
-            for e in range(2):
-                nc.vector.scalar_tensor_tensor(
-                    bent[e][:], square[:, e, :], 1.0, gh[2 * half + e][:], ALU.subtract, ALU.mult
-                )
+            return square
+
+        def finish(half, square):
+            bent = sb.tile([P, 2, Q], F32, name="bent%d" % half)
+            nc.vector.scalar_tensor_tensor(bent[:], square[:], 1.0, gh[half][:], ALU.subtract, ALU.mult)
             for e in range(2):
                 c = 2 * half + e
                 result = sb.tile([P, Q], F32, name="result%d" % c)
                 nc.vector.scalar_tensor_tensor(
-                    result[:], bent[e][:], neg_gain[:, c : c + 1], old_sb[:, c, :], ALU.mult, ALU.add
+                    result[:], bent[:, e, :], neg_gain[:, c : c + 1], old_sb[:, c, :], ALU.mult, ALU.add
                 )
                 nc.sync.dma_start(out[c * P : (c + 1) * P, :], result[:])
+
+        def query_half(half):
+            interleave(on_vector, wq_grouped[half][:, P * PACK :], wq_raw[half][:, :, P:HALF])
+            wq_q = quantize("wq%d" % half, wq_grouped[half])
+            return query_squares(half, [(wq_q, slice(0, P)), (wq_q, slice(P, HALF))])
+
+        dsc_grouped = grouped_tile("dsc_g", Q)
+        interleave(on_vector, dsc_grouped[:], dsc_raw[:])
+        dsc_q = quantize("dsc", dsc_grouped)
+        hs = [scaled_codes(0), scaled_codes(1)]
+        squares = []
+        for half in range(2):
+            squares.append(query_half(half))
+            hs.append(scaled_codes(2 + half))
+        for c in range(CHUNKS):
+            slot_sum(c, hs[c])
+        for half in range(2):
+            finish(half, squares[half])

@@ -19,6 +19,16 @@ P = 128
 PACK = 4
 CHUNKS = B // P
 HALF = B // 2
+MX_ALIGN = 64
+
+WORDS_AT = 0
+WI_AT = WORDS_AT + 4 * T
+QEMB_AT = WI_AT + 4 * PACK * HALF
+DSC_AT = QEMB_AT + 4 * PACK * Q
+WQ_AT = DSC_AT + 4 * PACK * Q
+OLD_AT = WQ_AT + 4 * PACK * B
+ISC_AT = OLD_AT + 4 * CHUNKS * Q
+LATE_BYTES = ISC_AT + 128
 
 
 def tile_attend_bsoftcodes_kernel(tc, qemb, wq, emb_words, emb_scales, wi, isc, dsc, gain, old, offs, out):
@@ -26,15 +36,17 @@ def tile_attend_bsoftcodes_kernel(tc, qemb, wq, emb_words, emb_scales, wi, isc, 
     with ExitStack() as ctx:
         sb = ctx.enter_context(tc.tile_pool(name="sb", bufs=1))
         ps = ctx.enter_context(tc.psum_pool(name="ps", bufs=1))
+        on_scalar, on_vector = nc.scalar.copy, nc.vector.tensor_copy
+        whole = slice(0, P)
+        chunk_of_half = [slice(0, P), slice(P, HALF)]
 
         def load_rows(pool, name, rows, offset=None):
-            width = rows.shape[1]
-            raw = pool.tile([P, PACK, width], F32, name=name, offset=offset)
+            raw = pool.tile([P, PACK, rows.shape[1]], F32, name=name, offset=offset)
             nc.sync.dma_start(raw[:], rows.rearrange("(p j) w -> p j w", j=PACK))
             return raw
 
         def grouped_tile(name, width):
-            return sb.tile([P, width * PACK], BF16, name=name, align_bytes=64)
+            return sb.tile([P, width * PACK], BF16, name=name, align_bytes=MX_ALIGN)
 
         def interleave(copy, grouped, raw):
             copy(
@@ -42,138 +54,148 @@ def tile_attend_bsoftcodes_kernel(tc, qemb, wq, emb_words, emb_scales, wi, isc, 
                 raw.rearrange("p j (c i) -> p c j i", i=2),
             )
 
-        on_scalar, on_vector = nc.scalar.copy, nc.vector.tensor_copy
-
         def quantize(name, grouped):
             width = grouped.shape[1] // PACK
-            codes = sb.tile([P, width], U32, name=name + "_codes", align_bytes=64)
-            scales = sb.tile([P, width], U8, name=name + "_scales", align_bytes=64)
-            nc.vector.quantize_mx(out=codes[:].bitcast(FP8X4), scales=scales[:], in_=grouped[:])
-            return codes, scales
+            words = sb.tile([P, width], U32, name=name + "_words", align_bytes=MX_ALIGN)
+            scales = sb.tile([P, width], U8, name=name + "_scales", align_bytes=MX_ALIGN)
+            nc.vector.quantize_mx(out=words[:].bitcast(FP8X4), scales=scales[:], in_=grouped[:])
+            return words, scales
 
-        def product(acc, left, left_cols, right, right_cols):
+        def product(acc, stationary, stationary_cols, moving, moving_cols):
             nc.tensor.matmul_mx(
                 out=acc,
-                lhsT=left[0][:, left_cols].bitcast(FP8X4),
-                lhsT_scale=left[1][:, left_cols],
-                rhs=right[0][:, right_cols].bitcast(FP8X4),
-                rhs_scale=right[1][:, right_cols],
+                lhsT=stationary[0][:, stationary_cols].bitcast(FP8X4),
+                lhsT_scale=stationary[1][:, stationary_cols],
+                rhs=moving[0][:, moving_cols].bitcast(FP8X4),
+                rhs_scale=moving[1][:, moving_cols],
                 start=True,
                 stop=True,
             )
 
-        whole = slice(0, P)
-
         offsets = sb.tile([P, I // 16], U16, name="offsets")
         nc.sync.dma_start(offsets[:], offs)
         wi_raw = [load_rows(sb, "wi_raw0", wi[:, 0:HALF])]
-        store_scales = sb.tile([P, T], U8, name="store_scales")
+        store_scales = sb.tile([P, T], U8, name="store_scales", align_bytes=MX_ALIGN, tag="wi0_words")
         nc.gpsimd.memset(store_scales[:].bitcast(I32), 0)
         for quad in range(4):
             nc.sync.dma_start(
                 store_scales[32 * quad : 32 * quad + 4, :].bitcast(I32),
                 emb_scales[0, 4 * quad : 4 * quad + 4, :].bitcast(I32),
             )
-        warm_in = sb.tile([P, 1], F32, name="warm_in")
-        nc.vector.memset(warm_in[:], 0.0)
-        warm_out = sb.tile([P, 1], F32, name="warm_out")
-        nc.scalar.activation(warm_out[:], warm_in[:], ACT.Tanh)
         gain_rows = sb.tile([P, P], F32, name="gain_rows")
         nc.vector.memset(gain_rows[:], 0.0)
         nc.scalar.dma_start(gain_rows[0:CHUNKS, :], gain.rearrange("(c p) o -> c (p o)", p=P))
 
         identity = sb.tile([P, P], F32, name="identity")
         late = ctx.enter_context(tc.tile_pool(name="late", bufs=1))
-        zeros = late.tile([P, 6688], F32, name="zeros", offset=0)
+        zeros = late.tile([P, LATE_BYTES // 4], F32, name="zeros", offset=0)
         nc.gpsimd.memset(zeros[:, 0:P], 0.0)
         nc.gpsimd.affine_select(
-            out=identity[:], in_=zeros[:, 0:P], compare_op=ALU.not_equal, fill=1.0,
-            base=0, pattern=[[-1, P]], channel_multiplier=1,
+            out=identity[:],
+            in_=zeros[:, 0:P],
+            compare_op=ALU.not_equal,
+            fill=1.0,
+            base=0,
+            pattern=[[-1, P]],
+            channel_multiplier=1,
         )
 
-        store_words = late.tile([P, T], U32, name="store_words", offset=0)
+        store_words = late.tile([P, T], U32, name="store_words", offset=WORDS_AT)
         nc.sync.dma_start(store_words[:].bitcast(I32), emb_words[0].rearrange("p n t -> p (n t)").bitcast(I32))
-        slot_scale = late.tile([P, PACK], F32, name="slot_scale", offset=26624)
-        nc.sync.dma_start(slot_scale[:], isc.rearrange("(p r) o -> p (r o)", r=PACK))
-        wi_raw.append(load_rows(late, "wi_raw1", wi[:, HALF:B], 8192))
-        qemb_raw = load_rows(late, "qemb_raw", qemb, 12288)
-        dsc_raw = load_rows(late, "dsc_raw", dsc, 14336)
-        wq_raw = [load_rows(late, "wq_raw%d" % h, wq[:, h * HALF : (h + 1) * HALF], 16384 + 4096 * h) for h in range(2)]
-        old_sb = late.tile([P, CHUNKS, Q], F32, name="old_sb", offset=24576)
+        slot_scale = late.tile([P, PACK], F32, name="slot_scale", offset=ISC_AT)
+        nc.sync.dma_start(slot_scale[:], isc.rearrange("(s r) o -> s (r o)", r=PACK))
+        wi_raw.append(load_rows(late, "wi_raw1", wi[:, HALF:B], WI_AT))
+        qemb_raw = load_rows(late, "qemb_raw", qemb, QEMB_AT)
+        wq_raw = [
+            load_rows(late, "wq_raw%d" % half, wq[:, half * HALF : (half + 1) * HALF], WQ_AT + 4 * PACK * HALF * half)
+            for half in range(2)
+        ]
+        dsc_raw = load_rows(late, "dsc_raw", dsc, DSC_AT)
+        old_sb = late.tile([P, CHUNKS, Q], F32, name="old_sb", offset=OLD_AT)
         nc.sync.dma_start(old_sb[:], old.rearrange("(c p) q -> p c q", p=P))
 
-        listed_scales = sb.tile([P, I], U8, name="listed_scales", align_bytes=64, tag="wi0_codes")
+        listed_scales = sb.tile([P, I], U8, name="listed_scales")
         nc.vector.tensor_copy(listed_scales[:], store_scales[:].indirect(offsets[:]))
-        dealt_scales = sb.tile([P, I], U8, name="dealt_scales", align_bytes=64)
+        wi_grouped = [grouped_tile("wi_grouped0", HALF)]
+        interleave(on_scalar, wi_grouped[0][:], wi_raw[0][:])
+        wi_first_half = quantize("wi0", wi_grouped[0])
+        dealt_scales = sb.tile([P, I], U8, name="dealt_scales", align_bytes=MX_ALIGN, tag="wi_grouped0")
         nc.vector.tensor_copy(
             dealt_scales[:].rearrange("p (r s) -> p r s", r=PACK),
             listed_scales[:].rearrange("p (s r) -> p r s", r=PACK),
         )
-        dealt_words = sb.tile([P, I], U32, name="dealt_words", align_bytes=64)
+        dealt_words = sb.tile([P, I], U32, name="dealt_words", align_bytes=MX_ALIGN)
         nc.vector.tensor_copy(
             dealt_words[:].rearrange("p (r s) -> p s r", r=PACK),
             store_words[:].indirect(offsets[:]),
         )
         items = (dealt_words, dealt_scales)
 
-        halves = [slice(0, P), slice(P, HALF)]
-        wi_grouped = [grouped_tile("wi_g0", HALF), grouped_tile("wi_g2", P), grouped_tile("wi_g3", P)]
-        interleave(on_scalar, wi_grouped[0][:], wi_raw[0][:])
+        wi_grouped.extend([grouped_tile("wi_grouped2", P), grouped_tile("wi_grouped3", P)])
         for e in range(2):
-            interleave(on_scalar, wi_grouped[1 + e][:], wi_raw[1][:, :, halves[e]])
-        wi_first = quantize("wi0", wi_grouped[0])
-        wi_q = [(wi_first, cols) for cols in halves]
-        wi_q.extend((quantize("wi%d" % (2 + e), wi_grouped[1 + e]), whole) for e in range(2))
-        qemb_grouped = grouped_tile("qemb_g", Q)
+            interleave(on_scalar, wi_grouped[1 + e][:], wi_raw[1][:, :, chunk_of_half[e]])
+        wi_mx = [(wi_first_half, cols) for cols in chunk_of_half]
+        wi_mx.extend((quantize("wi%d" % (2 + e), wi_grouped[1 + e]), whole) for e in range(2))
+        qemb_grouped = grouped_tile("qemb_grouped", Q)
         interleave(on_scalar, qemb_grouped[:], qemb_raw[:])
-        qemb_q = quantize("qemb", qemb_grouped)
+        qemb_mx = quantize("qemb", qemb_grouped)
 
-        gain_ps = ps.tile([P, P], F32, name="gain_ps")
-        nc.tensor.transpose(gain_ps[:], gain_rows[:], identity[:])
+        gain_turned = ps.tile([P, P], F32, name="gain_turned")
+        nc.tensor.transpose(gain_turned[:], gain_rows[:], identity[:])
         neg_gain = sb.tile([P, CHUNKS], F32, name="neg_gain")
-        nc.scalar.mul(neg_gain[:], gain_ps[:, 0:CHUNKS], -1.0)
+        nc.scalar.mul(neg_gain[:], gain_turned[:, 0:CHUNKS], -1.0)
 
-        wq_grouped = [grouped_tile("wq_g%d" % h, HALF) for h in range(2)]
-        codes_f32 = []
+        wq_grouped = [grouped_tile("wq_grouped%d" % half, HALF) for half in range(2)]
+        h1 = []
         for c in range(CHUNKS):
             if c % 2 == 0:
-                interleave(on_scalar, wq_grouped[c // 2][:, 0 : P * PACK], wq_raw[c // 2][:, :, 0:P])
-            bank = ps.tile([P, PACK, P], F32, name="g1_%d" % c, tag="bank%d" % c)
+                interleave(on_scalar, wq_grouped[c // 2][:, 0 : P * PACK], wq_raw[c // 2][:, :, chunk_of_half[0]])
+            g1 = ps.tile([P, PACK, P], F32, name="g1_%d" % c, tag="bank%d" % c)
             for r in range(PACK):
-                product(bank[:, r, :], items, slice(r * P, (r + 1) * P), *wi_q[c])
+                product(g1[:, r, :], items, slice(r * P, (r + 1) * P), *wi_mx[c])
             if c < 2:
-                h = late.tile([P, P, PACK], F32, name="h%d" % c, offset=8192 + 2048 * c)
+                h1_chunk = late.tile([P, P, PACK], F32, name="h1_%d" % c, offset=WI_AT + 4 * P * PACK * c)
             else:
-                h = sb.tile([P, P, PACK], F32, name="h%d" % c)
-            nc.scalar.activation(h[:], bank[:].rearrange("p r n -> p n r"), ACT.Tanh)
-            codes_f32.append(h)
+                h1_chunk = sb.tile([P, P, PACK], F32, name="h1_%d" % c)
+            nc.scalar.activation(h1_chunk[:], g1[:].rearrange("s r n -> s n r"), ACT.Tanh)
+            h1.append(h1_chunk)
 
         scale_spread = slot_scale[:].unsqueeze(1).to_broadcast([P, P, PACK])
         gh = [ps.tile([P, 2, Q], F32, name="gh_%d" % half, tag="bank%d" % half) for half in range(2)]
 
         def scaled_codes(c):
-            scaled = sb.tile([P, P * PACK], BF16, name="hs%d" % c, align_bytes=64)
+            hs_chunk = grouped_tile("hs_grouped%d" % c, P)
             nc.vector.tensor_tensor(
-                scaled[:].rearrange("p (n r) -> p n r", r=PACK), codes_f32[c][:], scale_spread, ALU.mult
+                hs_chunk[:].rearrange("s (n r) -> s n r", r=PACK), h1[c][:], scale_spread, ALU.mult
             )
-            return scaled
+            return hs_chunk
 
-        def slot_sum(c, scaled):
-            product(gh[c // 2][:, c % 2, :], quantize("hs%d" % c, scaled), whole, dsc_q, whole)
-
-        def query_squares(half, operands):
+        def squared_query_codes(half):
+            interleave(on_vector, wq_grouped[half][:, P * PACK :], wq_raw[half][:, :, chunk_of_half[1]])
+            wq_mx = quantize("wq%d" % half, wq_grouped[half])
             z = ps.tile([P, 2, Q], F32, name="z%d" % half)
             for e in range(2):
-                product(z[:, e, :], operands[e][0], operands[e][1], qemb_q, whole)
+                product(z[:, e, :], wq_mx, chunk_of_half[e], qemb_mx, whole)
             code = sb.tile([P, 2, Q], F32, name="code%d" % half)
             nc.scalar.activation(code[:], z[:], ACT.Tanh)
             square = sb.tile([P, 2, Q], F32, name="square%d" % half)
             nc.scalar.activation(square[:], code[:], ACT.Square)
             return square
 
-        def finish(half, square):
+        dsc_grouped = grouped_tile("dsc_grouped", Q)
+        interleave(on_scalar, dsc_grouped[:], dsc_raw[:])
+        dsc_mx = quantize("dsc", dsc_grouped)
+        hs = [scaled_codes(0), scaled_codes(1)]
+        squares = []
+        for half in range(2):
+            squares.append(squared_query_codes(half))
+            hs.append(scaled_codes(2 + half))
+        for c in range(CHUNKS):
+            product(gh[c // 2][:, c % 2, :], quantize("hs%d" % c, hs[c]), whole, dsc_mx, whole)
+
+        for half in range(2):
             bent = sb.tile([P, 2, Q], F32, name="bent%d" % half)
-            nc.vector.scalar_tensor_tensor(bent[:], square[:], 1.0, gh[half][:], ALU.subtract, ALU.mult)
+            nc.vector.scalar_tensor_tensor(bent[:], squares[half][:], 1.0, gh[half][:], ALU.subtract, ALU.mult)
             for e in range(2):
                 c = 2 * half + e
                 result = sb.tile([P, Q], F32, name="result%d" % c)
@@ -181,21 +203,3 @@ def tile_attend_bsoftcodes_kernel(tc, qemb, wq, emb_words, emb_scales, wi, isc, 
                     result[:], bent[:, e, :], neg_gain[:, c : c + 1], old_sb[:, c, :], ALU.mult, ALU.add
                 )
                 nc.sync.dma_start(out[c * P : (c + 1) * P, :], result[:])
-
-        def query_half(half):
-            interleave(on_vector, wq_grouped[half][:, P * PACK :], wq_raw[half][:, :, P:HALF])
-            wq_q = quantize("wq%d" % half, wq_grouped[half])
-            return query_squares(half, [(wq_q, slice(0, P)), (wq_q, slice(P, HALF))])
-
-        dsc_grouped = grouped_tile("dsc_g", Q)
-        interleave(on_vector, dsc_grouped[:], dsc_raw[:])
-        dsc_q = quantize("dsc", dsc_grouped)
-        hs = [scaled_codes(0), scaled_codes(1)]
-        squares = []
-        for half in range(2):
-            squares.append(query_half(half))
-            hs.append(scaled_codes(2 + half))
-        for c in range(CHUNKS):
-            slot_sum(c, hs[c])
-        for half in range(2):
-            finish(half, squares[half])

from contextlib import ExitStack

import concourse.mybir as mybir

K, B, T, I, Q = 512, 512, 2048, 512, 128
FLOPS = 2 * (K * B * Q + K * B * I + I * B * Q)

F32 = mybir.dt.float32
BF16 = mybir.dt.bfloat16
I32 = mybir.dt.int32
U32 = mybir.dt.uint32
U16 = mybir.dt.uint16
U8 = mybir.dt.uint8
FP8X4 = mybir.dt.float8_e4m3fn_x4
ACT = mybir.ActivationFunctionType
ALU = mybir.AluOpType

P = 128
PACK = 4
CHUNKS = B // P
HALF = B // 2
MX_ALIGN = 64

WORDS_AT = 0
WI_AT = WORDS_AT + 4 * T
QEMB_AT = WI_AT + 4 * PACK * HALF
DSC_AT = QEMB_AT + 4 * PACK * Q
WQ_AT = DSC_AT + 4 * PACK * Q
OLD_AT = WQ_AT + 4 * PACK * B
ISC_AT = OLD_AT + 4 * CHUNKS * Q
LATE_BYTES = ISC_AT + 128


def tile_attend_bsoftcodes_kernel(tc, qemb, wq, emb_words, emb_scales, wi, isc, dsc, gain, old, offs, out):
    nc = tc.nc
    with ExitStack() as ctx:
        sb = ctx.enter_context(tc.tile_pool(name="sb", bufs=1))
        ps = ctx.enter_context(tc.psum_pool(name="ps", bufs=1))
        on_scalar, on_vector = nc.scalar.copy, nc.vector.tensor_copy
        whole = slice(0, P)
        chunk_of_half = [slice(0, P), slice(P, HALF)]

        def load_rows(pool, name, rows, offset=None):
            raw = pool.tile([P, PACK, rows.shape[1]], F32, name=name, offset=offset)
            nc.sync.dma_start(raw[:], rows.rearrange("(p j) w -> p j w", j=PACK))
            return raw

        def grouped_tile(name, width):
            return sb.tile([P, width * PACK], BF16, name=name, align_bytes=MX_ALIGN)

        def interleave(copy, grouped, raw):
            copy(
                grouped.rearrange("p (c i j) -> p c j i", i=2, j=PACK),
                raw.rearrange("p j (c i) -> p c j i", i=2),
            )

        def quantize(name, grouped):
            width = grouped.shape[1] // PACK
            words = sb.tile([P, width], U32, name=name + "_words", align_bytes=MX_ALIGN)
            scales = sb.tile([P, width], U8, name=name + "_scales", align_bytes=MX_ALIGN)
            nc.vector.quantize_mx(out=words[:].bitcast(FP8X4), scales=scales[:], in_=grouped[:])
            return words, scales

        def product(acc, stationary, stationary_cols, moving, moving_cols):
            nc.tensor.matmul_mx(
                out=acc,
                lhsT=stationary[0][:, stationary_cols].bitcast(FP8X4),
                lhsT_scale=stationary[1][:, stationary_cols],
                rhs=moving[0][:, moving_cols].bitcast(FP8X4),
                rhs_scale=moving[1][:, moving_cols],
                start=True,
                stop=True,
            )

        offsets = sb.tile([P, I // 16], U16, name="offsets")
        nc.sync.dma_start(offsets[:], offs)
        wi_raw = [load_rows(sb, "wi_raw0", wi[:, 0:HALF])]
        store_scales = sb.tile([P, T], U8, name="store_scales", align_bytes=MX_ALIGN, tag="wi0_words")
        nc.gpsimd.memset(store_scales[:].bitcast(I32), 0)
        for quad in range(4):
            nc.sync.dma_start(
                store_scales[32 * quad : 32 * quad + 4, :].bitcast(I32),
                emb_scales[0, 4 * quad : 4 * quad + 4, :].bitcast(I32),
            )
        gain_rows = sb.tile([P, P], F32, name="gain_rows")
        nc.vector.memset(gain_rows[:], 0.0)
        nc.scalar.dma_start(gain_rows[0:CHUNKS, :], gain.rearrange("(c p) o -> c (p o)", p=P))

        identity = sb.tile([P, P], F32, name="identity")
        late = ctx.enter_context(tc.tile_pool(name="late", bufs=1))
        zeros = late.tile([P, LATE_BYTES // 4], F32, name="zeros", offset=0)
        nc.gpsimd.memset(zeros[:, 0:P], 0.0)
        nc.gpsimd.affine_select(
            out=identity[:],
            in_=zeros[:, 0:P],
            compare_op=ALU.not_equal,
            fill=1.0,
            base=0,
            pattern=[[-1, P]],
            channel_multiplier=1,
        )

        store_words = late.tile([P, T], U32, name="store_words", offset=WORDS_AT)
        nc.sync.dma_start(store_words[:].bitcast(I32), emb_words[0].rearrange("p n t -> p (n t)").bitcast(I32))
        slot_scale = late.tile([P, PACK], F32, name="slot_scale", offset=ISC_AT)
        nc.sync.dma_start(slot_scale[:], isc.rearrange("(s r) o -> s (r o)", r=PACK))
        wi_raw.append(load_rows(late, "wi_raw1", wi[:, HALF:B], WI_AT))
        qemb_raw = load_rows(late, "qemb_raw", qemb, QEMB_AT)
        wq_raw = [
            load_rows(late, "wq_raw%d" % half, wq[:, half * HALF : (half + 1) * HALF], WQ_AT + 4 * PACK * HALF * half)
            for half in range(2)
        ]
        dsc_raw = load_rows(late, "dsc_raw", dsc, DSC_AT)
        old_sb = late.tile([P, CHUNKS, Q], F32, name="old_sb", offset=OLD_AT)
        nc.sync.dma_start(old_sb[:], old.rearrange("(c p) q -> p c q", p=P))

        listed_scales = sb.tile([P, I], U8, name="listed_scales")
        nc.vector.tensor_copy(listed_scales[:], store_scales[:].indirect(offsets[:]))
        wi_grouped = [grouped_tile("wi_grouped0", HALF)]
        interleave(on_scalar, wi_grouped[0][:], wi_raw[0][:])
        wi_first_half = quantize("wi0", wi_grouped[0])
        dealt_scales = sb.tile([P, I], U8, name="dealt_scales", align_bytes=MX_ALIGN, tag="wi_grouped0")
        nc.vector.tensor_copy(
            dealt_scales[:].rearrange("p (r s) -> p r s", r=PACK),
            listed_scales[:].rearrange("p (s r) -> p r s", r=PACK),
        )
        dealt_words = sb.tile([P, I], U32, name="dealt_words", align_bytes=MX_ALIGN)
        nc.vector.tensor_copy(
            dealt_words[:].rearrange("p (r s) -> p s r", r=PACK),
            store_words[:].indirect(offsets[:]),
        )
        items = (dealt_words, dealt_scales)

        wi_grouped.extend([grouped_tile("wi_grouped2", P), grouped_tile("wi_grouped3", P)])
        for e in range(2):
            interleave(on_scalar, wi_grouped[1 + e][:], wi_raw[1][:, :, chunk_of_half[e]])
        wi_mx = [(wi_first_half, cols) for cols in chunk_of_half]
        wi_mx.extend((quantize("wi%d" % (2 + e), wi_grouped[1 + e]), whole) for e in range(2))
        qemb_grouped = grouped_tile("qemb_grouped", Q)
        interleave(on_scalar, qemb_grouped[:], qemb_raw[:])
        qemb_mx = quantize("qemb", qemb_grouped)

        gain_turned = ps.tile([P, P], F32, name="gain_turned")
        nc.tensor.transpose(gain_turned[:], gain_rows[:], identity[:])
        neg_gain = sb.tile([P, CHUNKS], F32, name="neg_gain")
        nc.scalar.mul(neg_gain[:], gain_turned[:, 0:CHUNKS], -1.0)

        wq_grouped = [grouped_tile("wq_grouped%d" % half, HALF) for half in range(2)]
        h1 = []
        for c in range(CHUNKS):
            if c % 2 == 0:
                interleave(on_scalar, wq_grouped[c // 2][:, 0 : P * PACK], wq_raw[c // 2][:, :, chunk_of_half[0]])
            g1 = ps.tile([P, PACK, P], F32, name="g1_%d" % c, tag="bank%d" % c)
            for r in range(PACK):
                product(g1[:, r, :], items, slice(r * P, (r + 1) * P), *wi_mx[c])
            if c < 2:
                h1_chunk = late.tile([P, P, PACK], F32, name="h1_%d" % c, offset=WI_AT + 4 * P * PACK * c)
            else:
                h1_chunk = sb.tile([P, P, PACK], F32, name="h1_%d" % c)
            nc.scalar.activation(h1_chunk[:], g1[:].rearrange("s r n -> s n r"), ACT.Tanh)
            h1.append(h1_chunk)

        scale_spread = slot_scale[:].unsqueeze(1).to_broadcast([P, P, PACK])
        gh = [ps.tile([P, 2, Q], F32, name="gh_%d" % half, tag="bank%d" % half) for half in range(2)]

        def scaled_codes(c):
            hs_chunk = grouped_tile("hs_grouped%d" % c, P)
            nc.vector.tensor_tensor(
                hs_chunk[:].rearrange("s (n r) -> s n r", r=PACK), h1[c][:], scale_spread, ALU.mult
            )
            return hs_chunk

        def squared_query_codes(half):
            interleave(on_vector, wq_grouped[half][:, P * PACK :], wq_raw[half][:, :, chunk_of_half[1]])
            wq_mx = quantize("wq%d" % half, wq_grouped[half])
            z = ps.tile([P, 2, Q], F32, name="z%d" % half)
            for e in range(2):
                product(z[:, e, :], wq_mx, chunk_of_half[e], qemb_mx, whole)
            code = sb.tile([P, 2, Q], F32, name="code%d" % half)
            nc.scalar.activation(code[:], z[:], ACT.Tanh)
            square = sb.tile([P, 2, Q], F32, name="square%d" % half)
            nc.scalar.activation(square[:], code[:], ACT.Square)
            return square

        dsc_grouped = grouped_tile("dsc_grouped", Q)
        interleave(on_scalar, dsc_grouped[:], dsc_raw[:])
        dsc_mx = quantize("dsc", dsc_grouped)
        hs = [scaled_codes(0), scaled_codes(1)]
        squares = []
        for half in range(2):
            squares.append(squared_query_codes(half))
            hs.append(scaled_codes(2 + half))
        for c in range(CHUNKS):
            product(gh[c // 2][:, c % 2, :], quantize("hs%d" % c, hs[c]), whole, dsc_mx, whole)

        for half in range(2):
            bent = sb.tile([P, 2, Q], F32, name="bent%d" % half)
            nc.vector.scalar_tensor_tensor(bent[:], squares[half][:], 1.0, gh[half][:], ALU.subtract, ALU.mult)
            for e in range(2):
                c = 2 * half + e
                result = sb.tile([P, Q], F32, name="result%d" % c)
                nc.vector.scalar_tensor_tensor(
                    result[:], bent[:, e, :], neg_gain[:, c : c + 1], old_sb[:, c, :], ALU.mult, ALU.add
                )
                nc.sync.dma_start(out[c * P : (c + 1) * P, :], result[:])
